import numpy as np
import ml_dtypes


def mxq(x, axis, fmt="e4m3"):
    dtype, down = {"e4m3": (ml_dtypes.float8_e4m3fn, 7), "e5m2": (ml_dtypes.float8_e5m2, 14)}[fmt]
    v = np.moveaxis(np.asarray(x, np.float32).astype(ml_dtypes.bfloat16).astype(np.float64), axis, -1)
    blocks = v.reshape(v.shape[:-1] + (-1, 32))
    amax = np.abs(blocks).max(-1, keepdims=True)
    byte = np.maximum(np.where(amax > 0, np.frexp(amax)[1] - 1 + 127, 0) - down, 1)
    scale = np.exp2(byte - 127.0)
    codes = (blocks / scale).astype(np.float32).astype(dtype).astype(np.float64)
    return np.moveaxis((codes * scale).reshape(v.shape), -1, axis)


WIDE = False


def mx_kscale(k):
    if not WIDE:
        return np.ones(k)
    levels = np.array([10, -10, 5, -5, 0])
    if k % 512:
        return np.exp2(np.random.permutation(np.resize(levels, k // 32))).repeat(32)
    a = np.empty((k // 512, 16))
    for p in range(k // 512):
        a[p, :8] = np.random.permutation(np.resize(levels, 8))
        for g in range(8):
            far = levels[np.abs(levels - a[p, g]) >= 10]
            a[p, g + 8] = far[np.random.randint(len(far))]
    return np.exp2(a.ravel()).repeat(32)


def f64(x):
    return np.asarray(x).astype(np.float64)


def striped(idx):
    return np.tile(idx.reshape(-1, 16).T, (8, 1)).astype(np.uint16)


def unstriped(offs):
    return offs[:16].T.reshape(-1).astype(np.int64)


def striped8(idx):
    return np.concatenate([x.reshape(-1, 16).T for x in idx]).astype(np.uint16)


def runs(offs, k):
    lists = np.stack([offs[16 * r : 16 * r + 16].T.reshape(-1) for r in range(8)]).astype(np.int64)
    return lists[np.arange(k) % 512 // 64]


def pack_weight(w):
    k, n = w.shape
    w = f64(np.asarray(w, np.float32).astype(ml_dtypes.bfloat16)).reshape(k // 32, 32, n)
    amax = np.abs(w).max(1)
    byte = np.clip(np.where(amax > 0, np.frexp(amax)[1] - 1 + 127 - 7, 1), 1, 254)
    scaled = (w * np.exp2(127.0 - byte)[:, None, :]).reshape(k, n).astype(np.float32)
    words = np.ascontiguousarray(scaled.reshape(k // 512, 128, 4, n).transpose(0, 1, 3, 2)).astype(ml_dtypes.float8_e4m3fn).view(np.uint8)
    return words, np.ascontiguousarray(byte.astype(np.uint8).reshape(k // 512, 16, n))


def unpack_weight(words, scales):
    g, p, n, _ = words.shape
    vals = np.ascontiguousarray(words).view(ml_dtypes.float8_e4m3fn).astype(np.float64) * np.repeat(np.exp2(scales.astype(np.float64) - 127.0), 8, axis=1)[..., None]
    return vals.transpose(0, 1, 3, 2).reshape(g * 512, n)

def planes(y):
    n, m = y.shape
    v = y.astype(np.float32).astype(ml_dtypes.bfloat16).astype(np.float64).reshape(n // 32, 32, m)
    top = np.abs(v).max(1)
    byte = np.clip(np.where(top > 0, np.frexp(top)[1] - 1 + 127 - 7, 1), 1, 254)
    codes = (v * np.exp2(127.0 - byte)[:, None, :]).reshape(n, m).astype(np.float32).astype(ml_dtypes.float8_e4m3fn).view(np.uint8)
    words = codes.reshape(n // 512, 128, 4, m).transpose(0, 1, 3, 2)
    return np.ascontiguousarray(words), np.ascontiguousarray(byte.astype(np.uint8).reshape(n // 512, 16, m))


K, T, S, G, H, W = 512, 1024, 512, 2048, 512, 256


def setup_inputs():
    n = np.random.standard_normal
    s = mx_kscale(K)[:, None]
    packed_xT = pack_weight(n((K, T)) * s)
    packed_dT = pack_weight(n((K, G)) / s)
    perm = np.stack([np.random.permutation(S) for _ in range(8)])
    perm2 = np.stack([np.random.permutation(S) for _ in range(8)])
    perm3 = np.stack([np.random.permutation(S) for _ in range(8)])
    return {
        "x_words": packed_xT[0],
        "x_scales": packed_xT[1],
        "d_words": packed_dT[0],
        "d_scales": packed_dT[1],
        "gs": (np.random.uniform(0.5, 1.5, (K, 1)) * s).astype(np.float32),
        "offs": striped(np.random.permutation(T)[:S]),
        "k1": striped8(np.random.randint(0, G, (8, H))),
        "hz": striped8(np.random.randint(0, T, (8, S))),
        "k2": striped8(np.random.randint(0, G, (8, H))),
        "n1": striped8(perm[:, :W]),
        "n2": striped8(perm[:, W:]),
        "n3": striped8(perm2[:, :W]),
        "n4": striped8(perm2[:, W:]),
        "n5": striped8(np.stack([np.random.permutation(S) for _ in range(8)])),
        "k3": striped8(np.random.randint(0, G, (8, H))),
        "k4": striped8(np.random.randint(0, G, (8, H))),
        "two": striped(np.random.permutation(T)[:S]),
        "k5": striped8(np.random.randint(0, G, (8, H))),
        "hy": striped8(np.random.randint(0, T, (8, S))),
        "n6": striped8(perm3[:, :W]),
        "n7": striped8(perm3[:, W:]),
        "n8": striped8(np.stack([np.random.permutation(S) for _ in range(8)])),
    }


def reference(x_words, x_scales, d_words, d_scales, gs, offs, k1, hz, k2, n1, n2, n3, n4, n5, k3, k4, two, k5, hy, n6, n7, n8):
    d_k3 = unpack_weight(d_words, d_scales)[np.arange(K)[:, None], runs(k3, K)]
    d_k1 = unpack_weight(d_words, d_scales)[np.arange(K)[:, None], runs(k1, K)]
    xq = unpack_weight(x_words, x_scales)[:, unstriped(offs)]
    d_k2 = unpack_weight(d_words, d_scales)[np.arange(K)[:, None], runs(k2, K)]
    x_hz = unpack_weight(x_words, x_scales)[np.arange(K)[:, None], runs(hz, K)]
    h = 0.0625 * (d_k1.T @ xq + d_k2.T @ x_hz)
    pa = h[np.arange(H)[:, None], runs(n1, H)]
    pb = h[np.arange(H)[:, None], runs(n2, H)]
    rb = np.minimum(pa, pb)
    ra = pa - pb
    ua = np.zeros((H, S))
    ua[np.arange(H)[:, None], runs(n3, H)] = ra
    ub = ua.copy()
    ub[np.arange(H)[:, None], runs(n4, H)] = rb
    z = f64(gs) * (np.maximum(ub, ub[np.arange(H)[:, None], runs(n5, H)]))
    d_k4 = unpack_weight(d_words, d_scales)[np.arange(K)[:, None], runs(k4, K)]
    x_two = unpack_weight(x_words, x_scales)[:, unstriped(two)]
    d_k5 = unpack_weight(d_words, d_scales)[np.arange(K)[:, None], runs(k5, K)]
    x_hy = unpack_weight(x_words, x_scales)[np.arange(K)[:, None], runs(hy, K)]
    h2 = 0.0625 * ((d_k3.T @ mxq(z, 0, "e4m3") + d_k4.T @ x_two + d_k5.T @ x_hy))
    pa2 = h2[np.arange(H)[:, None], runs(n6, H)]
    pb2 = h2[np.arange(H)[:, None], runs(n7, H)]
    rb2 = np.minimum(pa2, pb2)
    ra2 = np.maximum(pa2, pb2)
    ua2 = np.zeros((H, S))
    ua2[np.arange(H)[:, None], runs(n6, H)] = ra2
    ub2 = ua2.copy()
    ub2[np.arange(H)[:, None], runs(n7, H)] = rb2
    out_0 = ub2 - (ub2[np.arange(H)[:, None], runs(n8, H)])
    return (out_0,) + planes(out_0)

@@ -1,0 +1,264 @@
+from contextlib import ExitStack
+
+import concourse.mybir as mybir
+
+F32 = mybir.dt.float32
+BF16 = mybir.dt.bfloat16
+I32 = mybir.dt.int32
+U32 = mybir.dt.uint32
+U16 = mybir.dt.uint16
+U8 = mybir.dt.uint8
+FP8X4 = mybir.dt.float8_e4m3fn_x4
+ALU = mybir.AluOpType
+COPY = mybir.ActivationFunctionType.Copy
+
+P = 128
+PACK = 4
+S = 512
+W = 256
+T = 1024
+G = 2048
+FLOPS = 5 * 2 * 512 * 512 * 512
+
+
+def tile_picked_mthzmthcpgfordd_none_po_kernel(
+    tc, x_words, x_scales, d_words, d_scales, gs, offs, k1, hz, k2, n1, n2, n3, n4, n5,
+    k3, k4, two, k5, hy, n6, n7, n8, out_0, out_1, out_2,
+):
+    nc = tc.nc
+    with ExitStack() as ctx:
+        lists = ctx.enter_context(tc.tile_pool(name="lists", bufs=1))
+        keep = ctx.enter_context(tc.tile_pool(name="keep", bufs=1))
+        ring = ctx.enter_context(tc.tile_pool(name="ring", bufs=2))
+        psum = ctx.enter_context(tc.psum_pool(name="psum", bufs=1))
+
+        def load_list(name, src):
+            tile = lists.tile([P, src.shape[1]], U16, name=name)
+            nc.sync.dma_start(tile[:], src)
+            return tile
+
+        def held(name, width, dtype, tag=None):
+            return keep.tile([P, width], dtype, name=name, tag=tag or name, align_bytes=64)
+
+        def zeroed(name, width):
+            tile = held(name, width, U8)
+            nc.vector.memset(tile[:].bitcast(I32), 0)
+            return tile
+
+        def load_scales(tile, src):
+            nc.sync.dma_start(tile[0:P:8, :].bitcast(I32), src[0].bitcast(I32))
+
+        def load_words(name, src, width):
+            tile = held(name, width, U32)
+            nc.sync.dma_start(tile[:].bitcast(I32), src[0].rearrange("p n t -> p (n t)").bitcast(I32))
+            return tile
+
+        def gather(out, window, offsets):
+            nc.vector.tensor_copy(out, window[:].indirect(offsets[:]))
+
+        def place_rows(queue, dst, first_row, src):
+            for a in range(4):
+                queue.dma_start(dst[first_row + a : P : 32, :].bitcast(I32), src[8 * a : P : 32, :].bitcast(I32))
+
+        def deal(out, src):
+            nc.vector.tensor_copy(out.rearrange("p (l t m) -> p l m t", t=PACK, m=P), src.rearrange("p (l m t) -> p l m t", t=PACK, m=P))
+
+        def col(i):
+            return slice(i * S, (i + 1) * S)
+
+        def half(u):
+            return slice(u * W, (u + 1) * W)
+
+        xs_win = zeroed("xs_win", T)
+        ds_win = zeroed("ds_win", G)
+        l_offs = load_list("l_offs", offs)
+        xw_win = load_words("xw_win", x_words, T)
+        load_scales(xs_win, x_scales)
+        load_scales(ds_win, d_scales)
+        l_hz = load_list("l_hz", hz)
+        l_k1 = load_list("l_k1", k1)
+        l_k2 = load_list("l_k2", k2)
+        dw_win = load_words("dw_win", d_words, G)
+        l_k3 = load_list("l_k3", k3)
+        l_k4 = load_list("l_k4", k4)
+        l_k5 = load_list("l_k5", k5)
+        l_two = load_list("l_two", two)
+        l_hy = load_list("l_hy", hy)
+        l_n1 = load_list("l_n1", n1)
+        l_n2 = load_list("l_n2", n2)
+        l_n3 = load_list("l_n3", n3)
+        l_n4 = load_list("l_n4", n4)
+        l_n5 = load_list("l_n5", n5)
+        gain = held("gain", PACK, F32)
+        nc.sync.dma_start(gain[:], gs.rearrange("(p t) o -> p (t o)", t=PACK))
+        l_n6 = load_list("l_n6", n6)
+        l_n7 = load_list("l_n7", n7)
+        l_n8 = load_list("l_n8", n8)
+        placed_x1 = zeroed("placed_x1", 2 * S)
+        placed_d1 = zeroed("placed_d1", 2 * S)
+        placed_d2 = zeroed("placed_d2", S)
+        placed_x2 = zeroed("placed_x2", 2 * S)
+
+        xw1 = held("xw1", 2 * S, U32)
+        gather(xw1[:, col(0)], xw_win, l_offs)
+        gather(xw1[:, col(1)], xw_win, l_hz)
+        bytes_x1 = held("bytes_x1", 2 * S, U8)
+        gather(bytes_x1[:, col(0)], xs_win, l_offs)
+        gather(bytes_x1[:, col(1)], xs_win, l_hz)
+        place_rows(nc.scalar, placed_x1, 0, bytes_x1[:])
+        bytes_d1 = held("bytes_d1", 2 * S, U8)
+        gather(bytes_d1[:, col(0)], ds_win, l_k1)
+        gather(bytes_d1[:, col(1)], ds_win, l_k2)
+        ds1 = held("ds1", 2 * S, U8)
+        deal(ds1[:], bytes_d1[:])
+        place_rows(nc.scalar, placed_d1, 0, ds1[:])
+        dw1 = held("dw1", 2 * S, U32, tag="early")
+        gather(dw1[:, col(0)], dw_win, l_k1)
+        gather(dw1[:, col(1)], dw_win, l_k2)
+        dwd1 = held("dwd1", 2 * S, U32)
+        deal(dwd1[:], dw1[:])
+
+        def rows(i, t):
+            return slice(i * S + t * P, i * S + (t + 1) * P)
+
+        h = []
+        pa = []
+        npb = []
+        for t in range(PACK):
+            acc = psum.tile([P, S], F32, name="acc1_%d" % t)
+            for i in range(2):
+                nc.tensor.matmul_mx(
+                    out=acc[:], lhsT=dwd1[:, rows(i, t)].bitcast(FP8X4), lhsT_scale=placed_d1[:, rows(i, t)],
+                    rhs=xw1[:, col(i)].bitcast(FP8X4), rhs_scale=placed_x1[:, col(i)], start=(i == 0), stop=(i == 1),
+                )
+            h.append(held("h_%d" % t, S, F32))
+            nc.scalar.activation(h[t][:], acc[:], COPY, scale=0.0625)
+            pa.append(held("pa_%d" % t, W, F32))
+            npb.append(held("npb_%d" % t, W, F32))
+            nc.scalar.activation(pa[t][:], h[t][:].indirect(l_n1[:]), COPY)
+            nc.scalar.activation(npb[t][:], h[t][:].indirect(l_n2[:]), COPY, scale=-1.0)
+
+        bytes2 = held("bytes2", 5 * S, U8, tag="early")
+        for i, lst in enumerate((l_k3, l_k4, l_k5)):
+            gather(bytes2[:, col(i)], ds_win, lst)
+        gather(bytes2[:, col(3)], xs_win, l_two)
+        gather(bytes2[:, col(4)], xs_win, l_hy)
+        for i in range(3):
+            place_rows(nc.sync, placed_d2, 4 * i, bytes2[:, col(i)])
+        place_rows(nc.sync, placed_x2, 0, bytes2[:, 3 * S : 5 * S])
+        dw45 = held("dw45", 2 * S, U32)
+        gather(dw45[:, col(0)], dw_win, l_k4)
+        gather(dw45[:, col(1)], dw_win, l_k5)
+        dwd45 = held("dwd45", 2 * S, U32)
+        deal(dwd45[:], dw45[:])
+        xw_two = held("xw_two", S, U32)
+        gather(xw_two[:], xw_win, l_two)
+        ds2 = held("ds2", S, U8)
+        deal(ds2[:], placed_d2[:])
+
+        zb = held("zb", S * PACK, BF16)
+        zb3 = zb[:].rearrange("p (c t) -> p c t", t=PACK)
+        ub = {}
+
+        def scatter1(t):
+            rb = held("rb_%d" % t, W, F32, tag="late" if t == PACK - 1 else None)
+            nc.vector.scalar_tensor_tensor(rb[:], npb[t][:], -1.0, pa[t][:], ALU.mult, ALU.min)
+            ub[t] = ring.tile([P, S], F32, name="ub")
+            nc.vector.tensor_tensor(ub[t][:].indirect(l_n3[:]), pa[t][:], npb[t][:], ALU.add)
+            nc.vector.tensor_copy(ub[t][:].indirect(l_n4[:]), rb[:])
+
+        def finish1(t):
+            near = ring.tile([P, S], F32, name="near")
+            top = ring.tile([P, S], F32, name="top")
+            for u in range(2):
+                nc.scalar.activation(near[:, half(u)], ub[t][:].indirect(l_n5[:, 16 * u : 16 * u + 16]), COPY)
+            pieces = [half(0), half(1)] if t == PACK - 1 else [slice(0, S)]
+            for piece in pieces:
+                nc.vector.tensor_tensor(top[:, piece], ub[t][:, piece], near[:, piece], ALU.max)
+            for piece in pieces:
+                nc.scalar.activation(zb3[:, piece, t], top[:, piece], COPY, scale=gain[:, t : t + 1])
+
+        for t in range(PACK):
+            scatter1(t)
+            if t > 0:
+                finish1(t - 1)
+        finish1(PACK - 1)
+        late = held("late_words", 2 * S, U32, tag="late")
+        gather(late[:, col(0)], xw_win, l_hy)
+        gather(late[:, col(1)], dw_win, l_k3)
+        dwd3 = held("dwd3", S, U32)
+        deal(dwd3[:], late[:, col(1)])
+        z_words = held("z_words", S, U32)
+        z_scales = held("z_scales", S, U8)
+        for u in range(2):
+            nc.vector.quantize_mx(out=z_words[:, half(u)].bitcast(FP8X4), scales=z_scales[:, half(u)], in_=zb[:, u * W * PACK : (u + 1) * W * PACK])
+
+        acc2 = [psum.tile([P, S], F32, name="acc2_%d" % t) for t in range(PACK)]
+        for t in range(PACK):
+            nc.tensor.matmul_mx(
+                out=acc2[t][:], lhsT=dwd45[:, rows(0, t)].bitcast(FP8X4), lhsT_scale=ds2[4:P, rows(0, t)],
+                rhs=xw_two[:].bitcast(FP8X4), rhs_scale=placed_x2[:, col(0)], start=True, stop=False,
+            )
+        for t in range(PACK):
+            nc.tensor.matmul_mx(
+                out=acc2[t][:], lhsT=dwd45[:, rows(1, t)].bitcast(FP8X4), lhsT_scale=ds2[8:P, rows(0, t)],
+                rhs=late[:, col(0)].bitcast(FP8X4), rhs_scale=placed_x2[:, col(1)], start=False, stop=False,
+            )
+        for u in range(2):
+            for t in range(PACK):
+                nc.tensor.matmul_mx(
+                    out=acc2[t][:, half(u)], lhsT=dwd3[:, rows(0, t)].bitcast(FP8X4), lhsT_scale=ds2[:, rows(0, t)],
+                    rhs=z_words[:, half(u)].bitcast(FP8X4), rhs_scale=z_scales[:, half(u)], start=False, stop=(u == 1),
+                )
+
+        res = held("res", PACK * S, F32)
+        res3 = res[:].rearrange("p (t c) -> p c t", t=PACK)
+        ob = held("ob", S * PACK, BF16)
+        ob3 = ob[:].rearrange("p (c t) -> p c t", t=PACK)
+        out_rows = out_0.rearrange("(p t) j -> p t j", t=PACK)
+        ub2 = {}
+
+        def scatter2(t):
+            h2 = held("h2_%d" % t, S, F32)
+            nc.scalar.activation(h2[:], acc2[t][:], COPY, scale=0.0625)
+            pa2 = held("pa2_%d" % t, W, F32)
+            pb2 = held("pb2_%d" % t, W, F32)
+            if t == 0:
+                gather(pa2[:], h2, l_n6)
+            else:
+                nc.scalar.activation(pa2[:], h2[:].indirect(l_n6[:]), COPY)
+            nc.scalar.activation(pb2[:], h2[:].indirect(l_n7[:]), COPY)
+            ra2 = ring.tile([P, W], F32, name="ra2")
+            rb2 = ring.tile([P, W], F32, name="rb2")
+            nc.vector.tensor_tensor(ra2[:], pa2[:], pb2[:], ALU.max)
+            nc.vector.tensor_tensor(rb2[:], pa2[:], pb2[:], ALU.min)
+            ub2[t] = ring.tile([P, S], F32, name="ub2")
+            nc.vector.tensor_copy(ub2[t][:].indirect(l_n6[:]), ra2[:])
+            nc.vector.tensor_copy(ub2[t][:].indirect(l_n7[:]), rb2[:])
+
+        def finish2(t):
+            far = ring.tile([P, S], F32, name="far")
+            for u in range(2):
+                nc.scalar.activation(far[:, half(u)], ub2[t][:].indirect(l_n8[:, 16 * u : 16 * u + 16]), COPY)
+            pieces = [half(0), half(1)] if t == PACK - 1 else [slice(0, S)]
+            for piece in pieces:
+                here = res[:, t * S + piece.start : t * S + piece.stop]
+                nc.vector.tensor_tensor(here, ub2[t][:, piece], far[:, piece], ALU.subtract)
+                nc.sync.dma_start(out_rows[:, t, piece], here)
+
+        for t in range(PACK):
+            scatter2(t)
+            if t > 0:
+                finish2(t - 1)
+            if t == 2:
+                nc.scalar.copy(ob3[:, :, 0:2], res3[:, :, 0:2])
+        finish2(PACK - 1)
+        o_words = held("o_words", S, U32)
+        o_scales = held("o_scales", S, U8)
+        words_out = out_1[0].rearrange("p n t -> p (n t)").bitcast(I32)
+        for u in range(2):
+            nc.vector.tensor_copy(ob3[:, half(u), 2:4], res3[:, half(u), 2:4])
+            nc.vector.quantize_mx(out=o_words[:, half(u)].bitcast(FP8X4), scales=o_scales[:, half(u)], in_=ob[:, u * W * PACK : (u + 1) * W * PACK])
+            nc.sync.dma_start(words_out[:, half(u)], o_words[:, half(u)].bitcast(I32))
+        for q in range(4):
+            nc.scalar.dma_start(out_2[0, 4 * q : 4 * q + 4, :].bitcast(I32), o_scales[32 * q : 32 * q + 4, :].bitcast(I32))

@@ -1,6 +1,7 @@
 from contextlib import ExitStack
 
 import concourse.mybir as mybir
+from concourse.masks import make_identity
 
 F32 = mybir.dt.float32
 BF16 = mybir.dt.bfloat16
@@ -46,7 +47,7 @@ def tile_picked_mthzmthcpgfordd_none_po_kernel(
             return tile
 
         def load_scales(tile, src):
-            nc.sync.dma_start(tile[0:P:8, :].bitcast(I32), src[0].bitcast(I32))
+            nc.scalar.dma_start(tile[0:P:8, :].bitcast(I32), src[0].bitcast(I32))
 
         def load_words(name, src, width):
             tile = held(name, width, U32)
@@ -94,51 +95,53 @@ def tile_picked_mthzmthcpgfordd_none_po_kernel(
         l_n6 = load_list("l_n6", n6)
         l_n7 = load_list("l_n7", n7)
         l_n8 = load_list("l_n8", n8)
-        placed_x1 = zeroed("placed_x1", 2 * S)
-        placed_d1 = zeroed("placed_d1", 2 * S)
+        placed1 = zeroed("placed1", 4 * S)
+        ident = held("ident", P, F32)
+        make_identity(nc, ident[:])
         placed_d2 = zeroed("placed_d2", S)
         placed_x2 = zeroed("placed_x2", 2 * S)
 
+        bytes1 = held("bytes1", 4 * S, U8)
+        for i, (win, lst) in enumerate(((xs_win, l_offs), (xs_win, l_hz), (ds_win, l_k1), (ds_win, l_k2))):
+            gather(bytes1[:, col(i)], win, lst)
+        place_rows(nc.scalar, placed1, 0, bytes1[:])
         xw1 = held("xw1", 2 * S, U32)
         gather(xw1[:, col(0)], xw_win, l_offs)
         gather(xw1[:, col(1)], xw_win, l_hz)
-        bytes_x1 = held("bytes_x1", 2 * S, U8)
-        gather(bytes_x1[:, col(0)], xs_win, l_offs)
-        gather(bytes_x1[:, col(1)], xs_win, l_hz)
-        place_rows(nc.scalar, placed_x1, 0, bytes_x1[:])
-        bytes_d1 = held("bytes_d1", 2 * S, U8)
-        gather(bytes_d1[:, col(0)], ds_win, l_k1)
-        gather(bytes_d1[:, col(1)], ds_win, l_k2)
-        ds1 = held("ds1", 2 * S, U8)
-        deal(ds1[:], bytes_d1[:])
-        place_rows(nc.scalar, placed_d1, 0, ds1[:])
-        dw1 = held("dw1", 2 * S, U32, tag="early")
+        dw1 = held("dw1", 2 * S, U32)
         gather(dw1[:, col(0)], dw_win, l_k1)
         gather(dw1[:, col(1)], dw_win, l_k2)
-        dwd1 = held("dwd1", 2 * S, U32)
-        deal(dwd1[:], dw1[:])
 
         def rows(i, t):
             return slice(i * S + t * P, i * S + (t + 1) * P)
 
+        turned = []
+        for b in range(PACK):
+            acc = psum.tile([P, S], F32, name="acc1_%d" % b, tag="bank%d" % b)
+            for i in range(2):
+                nc.tensor.matmul_mx(
+                    out=acc[:], lhsT=xw1[:, rows(i, b)].bitcast(FP8X4), lhsT_scale=placed1[:, rows(i, b)],
+                    rhs=dw1[:, col(i)].bitcast(FP8X4), rhs_scale=placed1[:, col(2 + i)], start=(i == 0), stop=(i == 1),
+                )
+            turned.append(held("turned_%d" % b, S, F32))
+            nc.scalar.activation(
+                turned[b][:].rearrange("p (t m) -> p t m", t=PACK), acc[:].rearrange("p (m t) -> p t m", t=PACK), COPY, scale=0.0625
+            )
         h = []
         pa = []
         npb = []
         for t in range(PACK):
-            acc = psum.tile([P, S], F32, name="acc1_%d" % t)
-            for i in range(2):
-                nc.tensor.matmul_mx(
-                    out=acc[:], lhsT=dwd1[:, rows(i, t)].bitcast(FP8X4), lhsT_scale=placed_d1[:, rows(i, t)],
-                    rhs=xw1[:, col(i)].bitcast(FP8X4), rhs_scale=placed_x1[:, col(i)], start=(i == 0), stop=(i == 1),
-                )
+            back = psum.tile([P, S], F32, name="back_%d" % t, tag="bank%d" % (PACK + t))
+            for b in range(PACK):
+                nc.tensor.transpose(back[:, rows(0, b)], turned[b][:, rows(0, t)], ident[:])
             h.append(held("h_%d" % t, S, F32))
-            nc.scalar.activation(h[t][:], acc[:], COPY, scale=0.0625)
+            nc.scalar.copy(h[t][:], back[:])
             pa.append(held("pa_%d" % t, W, F32))
             npb.append(held("npb_%d" % t, W, F32))
             nc.scalar.activation(pa[t][:], h[t][:].indirect(l_n1[:]), COPY)
             nc.scalar.activation(npb[t][:], h[t][:].indirect(l_n2[:]), COPY, scale=-1.0)
 
-        bytes2 = held("bytes2", 5 * S, U8, tag="early")
+        bytes2 = held("bytes2", 5 * S, U8)
         for i, lst in enumerate((l_k3, l_k4, l_k5)):
             gather(bytes2[:, col(i)], ds_win, lst)
         gather(bytes2[:, col(3)], xs_win, l_two)
@@ -193,7 +196,7 @@ def tile_picked_mthzmthcpgfordd_none_po_kernel(
         for u in range(2):
             nc.vector.quantize_mx(out=z_words[:, half(u)].bitcast(FP8X4), scales=z_scales[:, half(u)], in_=zb[:, u * W * PACK : (u + 1) * W * PACK])
 
-        acc2 = [psum.tile([P, S], F32, name="acc2_%d" % t) for t in range(PACK)]
+        acc2 = [psum.tile([P, S], F32, name="acc2_%d" % t, tag="bank%d" % t) for t in range(PACK)]
         for t in range(PACK):
             nc.tensor.matmul_mx(
                 out=acc2[t][:], lhsT=dwd45[:, rows(0, t)].bitcast(FP8X4), lhsT_scale=ds2[4:P, rows(0, t)],
@@ -243,7 +246,8 @@ def tile_picked_mthzmthcpgfordd_none_po_kernel(
             pieces = [half(0), half(1)] if t == PACK - 1 else [slice(0, S)]
             for piece in pieces:
                 here = res[:, t * S + piece.start : t * S + piece.stop]
-                nc.vector.tensor_tensor(here, ub2[t][:, piece], far[:, piece], ALU.subtract)
+                engine = nc.vector if t == PACK - 1 else nc.gpsimd
+                engine.tensor_tensor(here, ub2[t][:, piece], far[:, piece], ALU.subtract)
                 nc.sync.dma_start(out_rows[:, t, piece], here)
 
         for t in range(PACK):

@@ -30,7 +30,6 @@ def tile_picked_mthzmthcpgfordd_none_po_kernel(
     with ExitStack() as ctx:
         lists = ctx.enter_context(tc.tile_pool(name="lists", bufs=1))
         keep = ctx.enter_context(tc.tile_pool(name="keep", bufs=1))
-        ring = ctx.enter_context(tc.tile_pool(name="ring", bufs=2))
         psum = ctx.enter_context(tc.psum_pool(name="psum", bufs=1))
 
         def load_list(name, src):
@@ -41,9 +40,9 @@ def tile_picked_mthzmthcpgfordd_none_po_kernel(
         def held(name, width, dtype, tag=None):
             return keep.tile([P, width], dtype, name=name, tag=tag or name, align_bytes=64)
 
-        def zeroed(name, width):
+        def zeroed(name, width, engine=nc.vector):
             tile = held(name, width, U8)
-            nc.vector.memset(tile[:].bitcast(I32), 0)
+            engine.memset(tile[:].bitcast(I32), 0)
             return tile
 
         def load_scales(tile, src):
@@ -70,15 +69,15 @@ def tile_picked_mthzmthcpgfordd_none_po_kernel(
         def half(u):
             return slice(u * W, (u + 1) * W)
 
-        xs_win = zeroed("xs_win", T)
+        xs_win = zeroed("xs_win", T, nc.gpsimd)
         ds_win = zeroed("ds_win", G)
         l_offs = load_list("l_offs", offs)
-        xw_win = load_words("xw_win", x_words, T)
         load_scales(xs_win, x_scales)
         load_scales(ds_win, d_scales)
         l_hz = load_list("l_hz", hz)
         l_k1 = load_list("l_k1", k1)
         l_k2 = load_list("l_k2", k2)
+        xw_win = load_words("xw_win", x_words, T)
         dw_win = load_words("dw_win", d_words, G)
         l_k3 = load_list("l_k3", k3)
         l_k4 = load_list("l_k4", k4)
@@ -128,18 +127,16 @@ def tile_picked_mthzmthcpgfordd_none_po_kernel(
                 turned[b][:].rearrange("p (t m) -> p t m", t=PACK), acc[:].rearrange("p (m t) -> p t m", t=PACK), COPY, scale=0.0625
             )
         h = []
-        pa = []
-        npb = []
+        pa = held("pa", PACK * W, F32)
+        npb = held("npb", PACK * W, F32)
         for t in range(PACK):
             back = psum.tile([P, S], F32, name="back_%d" % t, tag="bank%d" % (PACK + t))
             for b in range(PACK):
                 nc.tensor.transpose(back[:, rows(0, b)], turned[b][:, rows(0, t)], ident[:])
             h.append(held("h_%d" % t, S, F32))
             nc.scalar.copy(h[t][:], back[:])
-            pa.append(held("pa_%d" % t, W, F32))
-            npb.append(held("npb_%d" % t, W, F32))
-            nc.scalar.activation(pa[t][:], h[t][:].indirect(l_n1[:]), COPY)
-            nc.scalar.activation(npb[t][:], h[t][:].indirect(l_n2[:]), COPY, scale=-1.0)
+            nc.scalar.activation(pa[:, half(t)], h[t][:].indirect(l_n1[:]), COPY)
+            nc.scalar.activation(npb[:, half(t)], h[t][:].indirect(l_n2[:]), COPY, scale=-1.0)
 
         bytes2 = held("bytes2", 5 * S, U8)
         for i, lst in enumerate((l_k3, l_k4, l_k5)):
@@ -163,105 +160,155 @@ def tile_picked_mthzmthcpgfordd_none_po_kernel(
         zb3 = zb[:].rearrange("p (c t) -> p c t", t=PACK)
         ub = {}
 
-        def scatter1(t):
-            rb = held("rb_%d" % t, W, F32, tag="late" if t == PACK - 1 else None)
-            nc.vector.scalar_tensor_tensor(rb[:], npb[t][:], -1.0, pa[t][:], ALU.mult, ALU.min)
-            ub[t] = ring.tile([P, S], F32, name="ub")
-            nc.vector.tensor_tensor(ub[t][:].indirect(l_n3[:]), pa[t][:], npb[t][:], ALU.add)
-            nc.vector.tensor_copy(ub[t][:].indirect(l_n4[:]), rb[:])
+        near = {}
+        top = {}
 
-        def finish1(t):
-            near = ring.tile([P, S], F32, name="near")
-            top = ring.tile([P, S], F32, name="top")
+        def scatter_difference(t):
+            ub[t] = held("ub_%d" % t, S, F32, tag="near_%d" % (t - 2) if t >= 2 else None)
+            nc.vector.tensor_tensor(ub[t][:].indirect(l_n3[:]), pa[:, half(t)], npb[:, half(t)], ALU.add)
+
+        def scatter_smaller(t):
+            nc.vector.tensor_copy(ub[t][:].indirect(l_n4[:]), rb[:, half(t)])
+
+        def fetch_near(t):
             for u in range(2):
-                nc.scalar.activation(near[:, half(u)], ub[t][:].indirect(l_n5[:, 16 * u : 16 * u + 16]), COPY)
-            pieces = [half(0), half(1)] if t == PACK - 1 else [slice(0, S)]
-            for piece in pieces:
-                nc.vector.tensor_tensor(top[:, piece], ub[t][:, piece], near[:, piece], ALU.max)
-            for piece in pieces:
-                nc.scalar.activation(zb3[:, piece, t], top[:, piece], COPY, scale=gain[:, t : t + 1])
+                if t == PACK - 1:
+                    near[t, u] = held("near_%d_%d" % (t, u), W, F32)[:]
+                else:
+                    if u == 0:
+                        near[t] = held("near_%d" % t, S, F32)
+                    near[t, u] = near[t][:, half(u)]
+                nc.scalar.activation(near[t, u], ub[t][:].indirect(l_n5[:, 16 * u : 16 * u + 16]), COPY)
 
-        for t in range(PACK):
-            scatter1(t)
-            if t > 0:
-                finish1(t - 1)
-        finish1(PACK - 1)
-        late = held("late_words", 2 * S, U32, tag="late")
-        gather(late[:, col(0)], xw_win, l_hy)
-        gather(late[:, col(1)], dw_win, l_k3)
+        def pieces_of(t):
+            return [half(0), half(1)] if t == PACK - 1 else [slice(0, S)]
+
+        def larger(t):
+            top[t] = held("top_%d" % t, S, F32)
+            for u, piece in enumerate(pieces_of(t)):
+                other = near[t, u] if t == PACK - 1 else near[t][:]
+                nc.vector.tensor_tensor(top[t][:, piece], ub[t][:, piece], other, ALU.max)
+
+        def weigh(t):
+            for piece in pieces_of(t):
+                nc.scalar.activation(zb3[:, piece, t], top[t][:, piece], COPY, scale=gain[:, t : t + 1])
+
+        scatter_difference(0)
+        scatter_difference(1)
+        rb = held("rb", PACK * W, F32)
+        nc.vector.scalar_tensor_tensor(rb[:], npb[:], -1.0, pa[:], ALU.mult, ALU.min)
+        for t in (0, 1):
+            scatter_smaller(t)
+            fetch_near(t)
+        for t in (0, 1):
+            larger(t)
+            scatter_difference(t + 2)
+        for t in (0, 1):
+            weigh(t)
+        for t in (2, 3):
+            scatter_smaller(t)
+            fetch_near(t)
+        larger(2)
+        xw_hy = held("xw_hy", S, U32, tag="rb")
+        gather(xw_hy[:], xw_win, l_hy)
+        larger(3)
+        for t in (2, 3):
+            weigh(t)
+        dw3 = held("dw3", S, U32, tag="near_3_0")
+        gather(dw3[:], dw_win, l_k3)
         dwd3 = held("dwd3", S, U32)
-        deal(dwd3[:], late[:, col(1)])
+        deal(dwd3[:], dw3[:])
         z_words = held("z_words", S, U32)
         z_scales = held("z_scales", S, U8)
         for u in range(2):
             nc.vector.quantize_mx(out=z_words[:, half(u)].bitcast(FP8X4), scales=z_scales[:, half(u)], in_=zb[:, u * W * PACK : (u + 1) * W * PACK])
 
-        acc2 = [psum.tile([P, S], F32, name="acc2_%d" % t, tag="bank%d" % t) for t in range(PACK)]
-        for t in range(PACK):
-            nc.tensor.matmul_mx(
-                out=acc2[t][:], lhsT=dwd45[:, rows(0, t)].bitcast(FP8X4), lhsT_scale=ds2[4:P, rows(0, t)],
-                rhs=xw_two[:].bitcast(FP8X4), rhs_scale=placed_x2[:, col(0)], start=True, stop=False,
-            )
-        for t in range(PACK):
-            nc.tensor.matmul_mx(
-                out=acc2[t][:], lhsT=dwd45[:, rows(1, t)].bitcast(FP8X4), lhsT_scale=ds2[8:P, rows(0, t)],
-                rhs=late[:, col(0)].bitcast(FP8X4), rhs_scale=placed_x2[:, col(1)], start=False, stop=False,
-            )
-        for u in range(2):
-            for t in range(PACK):
+        groups = [(0, half(0)), (0, half(1))] + [(t, slice(0, S)) for t in range(1, PACK)]
+        acc2 = [
+            psum.tile([P, cols.stop - cols.start], F32, name="acc2_%d" % g, tag="bank%d" % g)
+            for g, (t, cols) in enumerate(groups)
+        ]
+        products = (
+            (dwd45[:, col(0)], 4, xw_two, placed_x2[:, col(0)]),
+            (dwd45[:, col(1)], 8, xw_hy, placed_x2[:, col(1)]),
+            (dwd3[:], 0, z_words, z_scales[:]),
+        )
+        for i, (d_codes, first_row, codes, scales) in enumerate(products):
+            for g, (t, cols) in enumerate(groups):
                 nc.tensor.matmul_mx(
-                    out=acc2[t][:, half(u)], lhsT=dwd3[:, rows(0, t)].bitcast(FP8X4), lhsT_scale=ds2[:, rows(0, t)],
-                    rhs=z_words[:, half(u)].bitcast(FP8X4), rhs_scale=z_scales[:, half(u)], start=False, stop=(u == 1),
+                    out=acc2[g][:], lhsT=d_codes[:, rows(0, t)].bitcast(FP8X4), lhsT_scale=ds2[first_row:P, rows(0, t)],
+                    rhs=codes[:, cols].bitcast(FP8X4), rhs_scale=scales[:, cols], start=(i == 0), stop=(i == 2),
                 )
 
-        res = held("res", PACK * S, F32)
-        res3 = res[:].rearrange("p (t c) -> p c t", t=PACK)
+        res = [[held("res_%d_%d" % (pair, u), 2 * W, F32) for u in range(2)] for pair in range(2)]
+
+        def round_pair(copy, pair, u):
+            copy(ob3[:, half(u), 2 * pair : 2 * pair + 2], res[pair][u][:].rearrange("p (t c) -> p c t", t=2))
+
         ob = held("ob", S * PACK, BF16)
         ob3 = ob[:].rearrange("p (c t) -> p c t", t=PACK)
         out_rows = out_0.rearrange("(p t) j -> p t j", t=PACK)
         ub2 = {}
+        fars = []
 
-        def scatter2(t):
-            h2 = held("h2_%d" % t, S, F32)
-            nc.scalar.activation(h2[:], acc2[t][:], COPY, scale=0.0625)
-            pa2 = held("pa2_%d" % t, W, F32)
-            pb2 = held("pb2_%d" % t, W, F32)
+        pa2 = held("pa2", PACK * W, F32)
+        pb2 = held("pb2", PACK * W, F32)
+        for t in range(PACK):
+            h2 = held("h2_%d" % t, S, F32, tag="h2")
+            for g, (owner, cols) in enumerate(groups):
+                if owner == t and g == 1:
+                    nc.vector.tensor_scalar(h2[:, cols], acc2[g][:], 0.0625, None, ALU.mult)
+                elif owner == t:
+                    nc.scalar.activation(h2[:, cols], acc2[g][:], COPY, scale=0.0625)
             if t == 0:
-                gather(pa2[:], h2, l_n6)
+                gather(pa2[:, half(t)], h2, l_n6)
             else:
-                nc.scalar.activation(pa2[:], h2[:].indirect(l_n6[:]), COPY)
-            nc.scalar.activation(pb2[:], h2[:].indirect(l_n7[:]), COPY)
-            ra2 = ring.tile([P, W], F32, name="ra2")
-            rb2 = ring.tile([P, W], F32, name="rb2")
-            nc.vector.tensor_tensor(ra2[:], pa2[:], pb2[:], ALU.max)
-            nc.vector.tensor_tensor(rb2[:], pa2[:], pb2[:], ALU.min)
-            ub2[t] = ring.tile([P, S], F32, name="ub2")
-            nc.vector.tensor_copy(ub2[t][:].indirect(l_n6[:]), ra2[:])
-            nc.vector.tensor_copy(ub2[t][:].indirect(l_n7[:]), rb2[:])
+                nc.scalar.activation(pa2[:, half(t)], h2[:].indirect(l_n6[:]), COPY)
+            nc.scalar.activation(pb2[:, half(t)], h2[:].indirect(l_n7[:]), COPY)
+        ra2 = held("ra2", PACK * W, F32)
+        rb2 = held("rb2", PACK * W, F32)
 
-        def finish2(t):
-            far = ring.tile([P, S], F32, name="far")
+        def extreme(out, op, first, last):
+            cols = slice(first * W, (last + 1) * W)
+            nc.vector.tensor_tensor(out[:, cols], pa2[:, cols], pb2[:, cols], op)
+
+        def scatter_larger(t):
+            ub2[t] = held("ub2_%d" % t, S, F32)
+            nc.vector.tensor_copy(ub2[t][:].indirect(l_n6[:]), ra2[:, half(t)])
+
+        def complete(t):
+            nc.vector.tensor_copy(ub2[t][:].indirect(l_n7[:]), rb2[:, half(t)])
+            if t % 2 == 0:
+                fars.append(held("far_%d" % t, 2 * S, F32, tag="h2" if t == 0 else "res_0_1"))
+            far = fars[t // 2][:, col(t % 2)]
+            engine = nc.vector if t == PACK - 1 else nc.gpsimd
             for u in range(2):
                 nc.scalar.activation(far[:, half(u)], ub2[t][:].indirect(l_n8[:, 16 * u : 16 * u + 16]), COPY)
-            pieces = [half(0), half(1)] if t == PACK - 1 else [slice(0, S)]
-            for piece in pieces:
-                here = res[:, t * S + piece.start : t * S + piece.stop]
-                engine = nc.vector if t == PACK - 1 else nc.gpsimd
-                engine.tensor_tensor(here, ub2[t][:, piece], far[:, piece], ALU.subtract)
-                nc.sync.dma_start(out_rows[:, t, piece], here)
+            for u in range(2):
+                here = res[t // 2][u][:, half(t % 2)]
+                engine.tensor_tensor(here, ub2[t][:, half(u)], far[:, half(u)], ALU.subtract)
+                nc.sync.dma_start(out_rows[:, t, half(u)], here)
 
-        for t in range(PACK):
-            scatter2(t)
-            if t > 0:
-                finish2(t - 1)
-            if t == 2:
-                nc.scalar.copy(ob3[:, :, 0:2], res3[:, :, 0:2])
-        finish2(PACK - 1)
+        extreme(ra2, ALU.max, 0, 0)
+        scatter_larger(0)
+        extreme(ra2, ALU.max, 1, 1)
+        extreme(rb2, ALU.min, 0, 1)
+        scatter_larger(1)
+        complete(0)
+        complete(1)
+        for u in range(2):
+            round_pair(nc.scalar.copy, 0, u)
+        extreme(ra2, ALU.max, 2, 3)
+        extreme(rb2, ALU.min, 2, 3)
+        scatter_larger(2)
+        scatter_larger(3)
+        complete(2)
+        complete(3)
         o_words = held("o_words", S, U32)
         o_scales = held("o_scales", S, U8)
         words_out = out_1[0].rearrange("p n t -> p (n t)").bitcast(I32)
         for u in range(2):
-            nc.vector.tensor_copy(ob3[:, half(u), 2:4], res3[:, half(u), 2:4])
+            round_pair(nc.vector.tensor_copy, 1, u)
             nc.vector.quantize_mx(out=o_words[:, half(u)].bitcast(FP8X4), scales=o_scales[:, half(u)], in_=ob[:, u * W * PACK : (u + 1) * W * PACK])
             nc.sync.dma_start(words_out[:, half(u)], o_words[:, half(u)].bitcast(I32))
         for q in range(4):

@@ -209,7 +209,7 @@ def tile_picked_mthzmthcpgfordd_none_po_kernel(
             scatter_smaller(t)
             fetch_near(t)
         larger(2)
-        xw_hy = held("xw_hy", S, U32, tag="rb")
+        xw_hy = held("xw_hy", S, U32, tag="near_2")
         gather(xw_hy[:], xw_win, l_hy)
         larger(3)
         for t in (2, 3):
@@ -312,4 +312,5 @@ def tile_picked_mthzmthcpgfordd_none_po_kernel(
             nc.vector.quantize_mx(out=o_words[:, half(u)].bitcast(FP8X4), scales=o_scales[:, half(u)], in_=ob[:, u * W * PACK : (u + 1) * W * PACK])
             nc.sync.dma_start(words_out[:, half(u)], o_words[:, half(u)].bitcast(I32))
         for q in range(4):
-            nc.scalar.dma_start(out_2[0, 4 * q : 4 * q + 4, :].bitcast(I32), o_scales[32 * q : 32 * q + 4, :].bitcast(I32))
+            queue = nc.scalar if q % 2 == 0 else nc.sync
+            queue.dma_start(out_2[0, 4 * q : 4 * q + 4, :].bitcast(I32), o_scales[32 * q : 32 * q + 4, :].bitcast(I32))

from contextlib import ExitStack

import concourse.mybir as mybir
from concourse.masks import make_identity

F32 = mybir.dt.float32
BF16 = mybir.dt.bfloat16
I32 = mybir.dt.int32
U32 = mybir.dt.uint32
U16 = mybir.dt.uint16
U8 = mybir.dt.uint8
FP8X4 = mybir.dt.float8_e4m3fn_x4
ALU = mybir.AluOpType
COPY = mybir.ActivationFunctionType.Copy

P = 128
PACK = 4
S = 512
W = 256
T = 1024
G = 2048
FLOPS = 5 * 2 * 512 * 512 * 512


def tile_picked_mthzmthcpgfordd_none_po_kernel(
    tc, x_words, x_scales, d_words, d_scales, gs, offs, k1, hz, k2, n1, n2, n3, n4, n5,
    k3, k4, two, k5, hy, n6, n7, n8, out_0, out_1, out_2,
):
    nc = tc.nc
    with ExitStack() as ctx:
        lists = ctx.enter_context(tc.tile_pool(name="lists", bufs=1))
        keep = ctx.enter_context(tc.tile_pool(name="keep", bufs=1))
        psum = ctx.enter_context(tc.psum_pool(name="psum", bufs=1))

        def load_list(name, src):
            tile = lists.tile([P, src.shape[1]], U16, name=name)
            nc.sync.dma_start(tile[:], src)
            return tile

        def held(name, width, dtype, tag=None):
            return keep.tile([P, width], dtype, name=name, tag=tag or name, align_bytes=64)

        def zeroed(name, width, engine=nc.vector):
            tile = held(name, width, U8)
            engine.memset(tile[:].bitcast(I32), 0)
            return tile

        def load_scales(tile, src):
            nc.scalar.dma_start(tile[0:P:8, :].bitcast(I32), src[0].bitcast(I32))

        def load_words(name, src, width):
            tile = held(name, width, U32)
            nc.sync.dma_start(tile[:].bitcast(I32), src[0].rearrange("p n t -> p (n t)").bitcast(I32))
            return tile

        def gather(out, window, offsets):
            nc.vector.tensor_copy(out, window[:].indirect(offsets[:]))

        def place_rows(queue, dst, first_row, src):
            for a in range(4):
                queue.dma_start(dst[first_row + a : P : 32, :].bitcast(I32), src[8 * a : P : 32, :].bitcast(I32))

        def deal(out, src):
            nc.vector.tensor_copy(out.rearrange("p (l t m) -> p l m t", t=PACK, m=P), src.rearrange("p (l m t) -> p l m t", t=PACK, m=P))

        def col(i):
            return slice(i * S, (i + 1) * S)

        def half(u):
            return slice(u * W, (u + 1) * W)

        xs_win = zeroed("xs_win", T, nc.gpsimd)
        ds_win = zeroed("ds_win", G)
        l_offs = load_list("l_offs", offs)
        load_scales(xs_win, x_scales)
        load_scales(ds_win, d_scales)
        l_hz = load_list("l_hz", hz)
        l_k1 = load_list("l_k1", k1)
        l_k2 = load_list("l_k2", k2)
        xw_win = load_words("xw_win", x_words, T)
        dw_win = load_words("dw_win", d_words, G)
        l_k3 = load_list("l_k3", k3)
        l_k4 = load_list("l_k4", k4)
        l_k5 = load_list("l_k5", k5)
        l_two = load_list("l_two", two)
        l_hy = load_list("l_hy", hy)
        l_n1 = load_list("l_n1", n1)
        l_n2 = load_list("l_n2", n2)
        l_n3 = load_list("l_n3", n3)
        l_n4 = load_list("l_n4", n4)
        l_n5 = load_list("l_n5", n5)
        gain = held("gain", PACK, F32)
        nc.sync.dma_start(gain[:], gs.rearrange("(p t) o -> p (t o)", t=PACK))
        l_n6 = load_list("l_n6", n6)
        l_n7 = load_list("l_n7", n7)
        l_n8 = load_list("l_n8", n8)
        placed1 = zeroed("placed1", 4 * S)
        ident = held("ident", P, F32)
        make_identity(nc, ident[:])
        placed_d2 = zeroed("placed_d2", S)
        placed_x2 = zeroed("placed_x2", 2 * S)

        bytes1 = held("bytes1", 4 * S, U8)
        for i, (win, lst) in enumerate(((xs_win, l_offs), (xs_win, l_hz), (ds_win, l_k1), (ds_win, l_k2))):
            gather(bytes1[:, col(i)], win, lst)
        place_rows(nc.scalar, placed1, 0, bytes1[:])
        xw1 = held("xw1", 2 * S, U32)
        gather(xw1[:, col(0)], xw_win, l_offs)
        gather(xw1[:, col(1)], xw_win, l_hz)
        dw1 = held("dw1", 2 * S, U32)
        gather(dw1[:, col(0)], dw_win, l_k1)
        gather(dw1[:, col(1)], dw_win, l_k2)

        def rows(i, t):
            return slice(i * S + t * P, i * S + (t + 1) * P)

        turned = []
        for b in range(PACK):
            acc = psum.tile([P, S], F32, name="acc1_%d" % b, tag="bank%d" % b)
            for i in range(2):
                nc.tensor.matmul_mx(
                    out=acc[:], lhsT=xw1[:, rows(i, b)].bitcast(FP8X4), lhsT_scale=placed1[:, rows(i, b)],
                    rhs=dw1[:, col(i)].bitcast(FP8X4), rhs_scale=placed1[:, col(2 + i)], start=(i == 0), stop=(i == 1),
                )
            turned.append(held("turned_%d" % b, S, F32))
            nc.scalar.activation(
                turned[b][:].rearrange("p (t m) -> p t m", t=PACK), acc[:].rearrange("p (m t) -> p t m", t=PACK), COPY, scale=0.0625
            )
        h = []
        pa = held("pa", PACK * W, F32)
        npb = held("npb", PACK * W, F32)
        for t in range(PACK):
            back = psum.tile([P, S], F32, name="back_%d" % t, tag="bank%d" % (PACK + t))
            for b in range(PACK):
                nc.tensor.transpose(back[:, rows(0, b)], turned[b][:, rows(0, t)], ident[:])
            h.append(held("h_%d" % t, S, F32))
            nc.scalar.copy(h[t][:], back[:])
            nc.scalar.activation(pa[:, half(t)], h[t][:].indirect(l_n1[:]), COPY)
            nc.scalar.activation(npb[:, half(t)], h[t][:].indirect(l_n2[:]), COPY, scale=-1.0)

        bytes2 = held("bytes2", 5 * S, U8)
        for i, lst in enumerate((l_k3, l_k4, l_k5)):
            gather(bytes2[:, col(i)], ds_win, lst)
        gather(bytes2[:, col(3)], xs_win, l_two)
        gather(bytes2[:, col(4)], xs_win, l_hy)
        for i in range(3):
            place_rows(nc.sync, placed_d2, 4 * i, bytes2[:, col(i)])
        place_rows(nc.sync, placed_x2, 0, bytes2[:, 3 * S : 5 * S])
        dw45 = held("dw45", 2 * S, U32)
        gather(dw45[:, col(0)], dw_win, l_k4)
        gather(dw45[:, col(1)], dw_win, l_k5)
        dwd45 = held("dwd45", 2 * S, U32)
        deal(dwd45[:], dw45[:])
        xw_two = held("xw_two", S, U32)
        gather(xw_two[:], xw_win, l_two)
        ds2 = held("ds2", S, U8)
        deal(ds2[:], placed_d2[:])

        zb = held("zb", S * PACK, BF16)
        zb3 = zb[:].rearrange("p (c t) -> p c t", t=PACK)
        ub = {}

        near = {}
        top = {}

        def scatter_difference(t):
            ub[t] = held("ub_%d" % t, S, F32, tag="near_%d" % (t - 2) if t >= 2 else None)
            nc.vector.tensor_tensor(ub[t][:].indirect(l_n3[:]), pa[:, half(t)], npb[:, half(t)], ALU.add)

        def scatter_smaller(t):
            nc.vector.tensor_copy(ub[t][:].indirect(l_n4[:]), rb[:, half(t)])

        def fetch_near(t):
            for u in range(2):
                if t == PACK - 1:
                    near[t, u] = held("near_%d_%d" % (t, u), W, F32)[:]
                else:
                    if u == 0:
                        near[t] = held("near_%d" % t, S, F32)
                    near[t, u] = near[t][:, half(u)]
                nc.scalar.activation(near[t, u], ub[t][:].indirect(l_n5[:, 16 * u : 16 * u + 16]), COPY)

        def pieces_of(t):
            return [half(0), half(1)] if t == PACK - 1 else [slice(0, S)]

        def larger(t):
            top[t] = held("top_%d" % t, S, F32)
            for u, piece in enumerate(pieces_of(t)):
                other = near[t, u] if t == PACK - 1 else near[t][:]
                nc.vector.tensor_tensor(top[t][:, piece], ub[t][:, piece], other, ALU.max)

        def weigh(t):
            for piece in pieces_of(t):
                nc.scalar.activation(zb3[:, piece, t], top[t][:, piece], COPY, scale=gain[:, t : t + 1])

        scatter_difference(0)
        scatter_difference(1)
        rb = held("rb", PACK * W, F32)
        nc.vector.scalar_tensor_tensor(rb[:], npb[:], -1.0, pa[:], ALU.mult, ALU.min)
        for t in (0, 1):
            scatter_smaller(t)
            fetch_near(t)
        for t in (0, 1):
            larger(t)
            scatter_difference(t + 2)
        for t in (0, 1):
            weigh(t)
        for t in (2, 3):
            scatter_smaller(t)
            fetch_near(t)
        larger(2)
        xw_hy = held("xw_hy", S, U32, tag="near_2")
        gather(xw_hy[:], xw_win, l_hy)
        larger(3)
        for t in (2, 3):
            weigh(t)
        dw3 = held("dw3", S, U32, tag="near_3_0")
        gather(dw3[:], dw_win, l_k3)
        dwd3 = held("dwd3", S, U32)
        deal(dwd3[:], dw3[:])
        z_words = held("z_words", S, U32)
        z_scales = held("z_scales", S, U8)
        for u in range(2):
            nc.vector.quantize_mx(out=z_words[:, half(u)].bitcast(FP8X4), scales=z_scales[:, half(u)], in_=zb[:, u * W * PACK : (u + 1) * W * PACK])

        groups = [(0, half(0)), (0, half(1))] + [(t, slice(0, S)) for t in range(1, PACK)]
        acc2 = [
            psum.tile([P, cols.stop - cols.start], F32, name="acc2_%d" % g, tag="bank%d" % g)
            for g, (t, cols) in enumerate(groups)
        ]
        products = (
            (dwd45[:, col(0)], 4, xw_two, placed_x2[:, col(0)]),
            (dwd45[:, col(1)], 8, xw_hy, placed_x2[:, col(1)]),
            (dwd3[:], 0, z_words, z_scales[:]),
        )
        for i, (d_codes, first_row, codes, scales) in enumerate(products):
            for g, (t, cols) in enumerate(groups):
                nc.tensor.matmul_mx(
                    out=acc2[g][:], lhsT=d_codes[:, rows(0, t)].bitcast(FP8X4), lhsT_scale=ds2[first_row:P, rows(0, t)],
                    rhs=codes[:, cols].bitcast(FP8X4), rhs_scale=scales[:, cols], start=(i == 0), stop=(i == 2),
                )

        res = [[held("res_%d_%d" % (pair, u), 2 * W, F32) for u in range(2)] for pair in range(2)]

        def round_pair(copy, pair, u):
            copy(ob3[:, half(u), 2 * pair : 2 * pair + 2], res[pair][u][:].rearrange("p (t c) -> p c t", t=2))

        ob = held("ob", S * PACK, BF16)
        ob3 = ob[:].rearrange("p (c t) -> p c t", t=PACK)
        out_rows = out_0.rearrange("(p t) j -> p t j", t=PACK)
        ub2 = {}
        fars = []

        pa2 = held("pa2", PACK * W, F32)
        pb2 = held("pb2", PACK * W, F32)
        for t in range(PACK):
            h2 = held("h2_%d" % t, S, F32, tag="h2")
            for g, (owner, cols) in enumerate(groups):
                if owner == t and g == 1:
                    nc.vector.tensor_scalar(h2[:, cols], acc2[g][:], 0.0625, None, ALU.mult)
                elif owner == t:
                    nc.scalar.activation(h2[:, cols], acc2[g][:], COPY, scale=0.0625)
            if t == 0:
                gather(pa2[:, half(t)], h2, l_n6)
            else:
                nc.scalar.activation(pa2[:, half(t)], h2[:].indirect(l_n6[:]), COPY)
            nc.scalar.activation(pb2[:, half(t)], h2[:].indirect(l_n7[:]), COPY)
        ra2 = held("ra2", PACK * W, F32)
        rb2 = held("rb2", PACK * W, F32)

        def extreme(out, op, first, last):
            cols = slice(first * W, (last + 1) * W)
            nc.vector.tensor_tensor(out[:, cols], pa2[:, cols], pb2[:, cols], op)

        def scatter_larger(t):
            ub2[t] = held("ub2_%d" % t, S, F32)
            nc.vector.tensor_copy(ub2[t][:].indirect(l_n6[:]), ra2[:, half(t)])

        def complete(t):
            nc.vector.tensor_copy(ub2[t][:].indirect(l_n7[:]), rb2[:, half(t)])
            if t % 2 == 0:
                fars.append(held("far_%d" % t, 2 * S, F32, tag="h2" if t == 0 else "res_0_1"))
            far = fars[t // 2][:, col(t % 2)]
            engine = nc.vector if t == PACK - 1 else nc.gpsimd
            for u in range(2):
                nc.scalar.activation(far[:, half(u)], ub2[t][:].indirect(l_n8[:, 16 * u : 16 * u + 16]), COPY)
            for u in range(2):
                here = res[t // 2][u][:, half(t % 2)]
                engine.tensor_tensor(here, ub2[t][:, half(u)], far[:, half(u)], ALU.subtract)
                nc.sync.dma_start(out_rows[:, t, half(u)], here)

        extreme(ra2, ALU.max, 0, 0)
        scatter_larger(0)
        extreme(ra2, ALU.max, 1, 1)
        extreme(rb2, ALU.min, 0, 1)
        scatter_larger(1)
        complete(0)
        complete(1)
        for u in range(2):
            round_pair(nc.scalar.copy, 0, u)
        extreme(ra2, ALU.max, 2, 3)
        extreme(rb2, ALU.min, 2, 3)
        scatter_larger(2)
        scatter_larger(3)
        complete(2)
        complete(3)
        o_words = held("o_words", S, U32)
        o_scales = held("o_scales", S, U8)
        words_out = out_1[0].rearrange("p n t -> p (n t)").bitcast(I32)
        for u in range(2):
            round_pair(nc.vector.tensor_copy, 1, u)
            nc.vector.quantize_mx(out=o_words[:, half(u)].bitcast(FP8X4), scales=o_scales[:, half(u)], in_=ob[:, u * W * PACK : (u + 1) * W * PACK])
            nc.sync.dma_start(words_out[:, half(u)], o_words[:, half(u)].bitcast(I32))
        for q in range(4):
            queue = nc.scalar if q % 2 == 0 else nc.sync
            queue.dma_start(out_2[0, 4 * q : 4 * q + 4, :].bitcast(I32), o_scales[32 * q : 32 * q + 4, :].bitcast(I32))
